import numpy as np
import ml_dtypes


def mxq(x, axis, fmt="e4m3"):
    dtype, down = {"e4m3": (ml_dtypes.float8_e4m3fn, 7), "e5m2": (ml_dtypes.float8_e5m2, 14)}[fmt]
    v = np.moveaxis(np.asarray(x, np.float32).astype(ml_dtypes.bfloat16).astype(np.float64), axis, -1)
    blocks = v.reshape(v.shape[:-1] + (-1, 32))
    amax = np.abs(blocks).max(-1, keepdims=True)
    byte = np.maximum(np.where(amax > 0, np.frexp(amax)[1] - 1 + 127, 0) - down, 1)
    scale = np.exp2(byte - 127.0)
    codes = (blocks / scale).astype(np.float32).astype(dtype).astype(np.float64)
    return np.moveaxis((codes * scale).reshape(v.shape), -1, axis)


WIDE = False


def mx_kscale(k):
    if not WIDE:
        return np.ones(k)
    levels = np.array([10, -10, 5, -5, 0])
    if k % 512:
        return np.exp2(np.random.permutation(np.resize(levels, k // 32))).repeat(32)
    a = np.empty((k // 512, 16))
    for p in range(k // 512):
        a[p, :8] = np.random.permutation(np.resize(levels, 8))
        for g in range(8):
            far = levels[np.abs(levels - a[p, g]) >= 10]
            a[p, g + 8] = far[np.random.randint(len(far))]
    return np.exp2(a.ravel()).repeat(32)


def f64(x):
    return np.asarray(x).astype(np.float64)


def striped(idx):
    return np.tile(np.asarray(idx).reshape(-1, 16).T, (8, 1)).astype(np.uint16)


def unstriped(offs):
    return offs[:16].T.reshape(-1).astype(np.int64)


E2M1 = np.array([0.0, 0.5, 1.0, 1.5, 2.0, 3.0, 4.0, 6.0, -0.0, -0.5, -1.0, -1.5, -2.0, -3.0, -4.0, -6.0])


def pack_weight(w, fmt):
    k, n = w.shape
    w = f64(np.asarray(w, np.float32).astype(ml_dtypes.bfloat16)).reshape(k // 32, 32, n)
    amax = np.abs(w).max(1)
    if fmt == "e4m3":
        byte = np.frexp(amax)[1] - 1 + 127 - 7
    else:
        mant, ex = np.frexp(amax / 6.0)
        byte = np.where(mant > 0.5, ex, ex - 1) + 127
    byte = np.clip(np.where(amax > 0, byte, 1), 1, 254)
    scaled = (w * np.exp2(127.0 - byte)[:, None, :]).reshape(k, n).astype(np.float32)
    by_word = np.ascontiguousarray(scaled.reshape(k // 512, 128, 4, n).transpose(0, 1, 3, 2))
    if fmt == "e4m3":
        words = by_word.astype(ml_dtypes.float8_e4m3fn).view(np.uint8)
    else:
        c = by_word.astype(ml_dtypes.float4_e2m1fn).view(np.uint8) & 0xF
        words = (c[..., 0::2] | (c[..., 1::2] << 4)).reshape(k // 512, 128, 2 * n)
    return np.ascontiguousarray(words), np.ascontiguousarray(byte.astype(np.uint8).reshape(k // 512, 16, n))


def unpack_weight(words, scales, fmt):
    g, _, n = scales.shape
    words = np.ascontiguousarray(words).reshape(g, 128, n, -1)
    if fmt == "e4m3":
        vals = words.view(ml_dtypes.float8_e4m3fn).astype(np.float64)
    else:
        nib = np.empty((g, 128, n, 4), np.uint8)
        nib[..., 0::2] = words & 0xF
        nib[..., 1::2] = words >> 4
        vals = E2M1[nib]
    vals = vals * np.repeat(np.exp2(scales.astype(np.float64) - 127.0), 8, axis=1)[..., None]
    return vals.transpose(0, 1, 3, 2).reshape(g * 512, n)


D, T, I, J, U, Z, E = 512, 2048, 512, 512, 1024, 1024, 512


def setup_inputs():
    n = np.random.standard_normal
    idx = np.random.permutation(T)[:I]
    idx2 = np.random.permutation(U)[:J]
    idx3 = np.random.permutation(Z)[:J]
    fd = mx_kscale(D)
    fi = mx_kscale(I)
    ti = np.ones(T)
    ti[idx] = fi
    keysp = pack_weight(n((D, T)) / fd[:, None], "e4m3")
    return {
        "keys_words": keysp[0],
        "keys_scales": keysp[1],
        "notes": (n((D, U)) * 1.0 / np.sqrt(D) * fd[:, None]).astype(np.float32),
        "users2": (n((D, Z)) * 1.0 / np.sqrt(D) * fd[:, None]).astype(np.float32),
        "rowf": (np.random.uniform(0.02, 0.08, (I, 1)) * fi[:, None]).astype(np.float32),
        "vals": (n((E, T)) / ti).astype(np.float32),
        "mem": (np.random.uniform(0.3, 1.0, (1, J))).astype(np.float32),
        "offs": striped(idx),
        "offs2": striped(idx2),
        "offs3": striped(idx3),
    }


def reference(keys_words, keys_scales, notes, users2, rowf, vals, mem, offs, offs2, offs3):
    idx = unstriped(offs)
    idx2 = unstriped(offs2)
    idx3 = unstriped(offs3)
    keysu = unpack_weight(keys_words, keys_scales, "e4m3")
    keysidxg = keysu[:, idx]
    notesq = mxq(f64(notes), 0, "e4m3")
    g1 = keysidxg.T @ notesq
    users2idx3q = mxq(f64(users2)[:, idx3], 0, "e4m3")
    g2 = keysidxg.T @ users2idx3q
    g0 = np.maximum(g1[:, idx2], g2)
    gr1 = g0 * f64(rowf)
    vt1 = f64(vals)[:, idx].T
    vt1q = mxq(vt1, 0, "e4m3")
    gr1q = mxq(gr1, 0, "e4m3")
    o = vt1q.T @ gr1q
    o1 = np.pad(o, ((0, 0), (1, 0)))[:, :J]
    y = o - o1 * f64(mem)
    return y

@@ -1,0 +1,176 @@
+from contextlib import ExitStack
+
+import concourse.mybir as mybir
+from concourse.masks import make_identity
+
+D, T, I, J, U, Z, E = 512, 2048, 512, 512, 1024, 1024, 512
+FLOPS = 2 * D * I * U + 2 * D * I * J + 2 * I * E * J
+
+F32 = mybir.dt.float32
+BF16 = mybir.dt.bfloat16
+I32 = mybir.dt.int32
+U32 = mybir.dt.uint32
+U16 = mybir.dt.uint16
+U8 = mybir.dt.uint8
+FP8X4 = mybir.dt.float8_e4m3fn_x4
+ALU = mybir.AluOpType
+COPY = mybir.ActivationFunctionType.Copy
+
+P = 128
+PACK = 4
+BANK = 512
+
+
+def woven(grouped):
+    return grouped.rearrange("p (c i) t -> p c t i", i=4)
+
+
+def by_planes(planes):
+    return planes.rearrange("p t (c i) -> p c t i", i=4)
+
+
+def tile_attend_tab_wideandown_changes_kernel(
+    tc, keys_words, keys_scales, notes, users2, rowf, vals, mem, offs, offs2, offs3, out
+):
+    nc = tc.nc
+    with ExitStack() as ctx:
+        keep = ctx.enter_context(tc.tile_pool(name="keep", bufs=1))
+        psum = ctx.enter_context(tc.psum_pool(name="psum", bufs=1))
+
+        def quantise(name, grouped, cols, tag=""):
+            codes = keep.tile([P, cols], U32, name=name + "_codes", tag=tag, align_bytes=64)
+            scales = keep.tile([P, cols], U8, name=name + "_scales", align_bytes=64)
+            nc.vector.quantize_mx(out=codes[:].bitcast(FP8X4), scales=scales[:], in_=grouped)
+            return codes, scales
+
+        landed = keep.tile([P, T // 4], I32, name="landed")
+        for q in range(4):
+            nc.sync.dma_start(
+                out=landed[32 * q : 32 * q + 4, :],
+                in_=keys_scales[0][4 * q : 4 * q + 4, :].bitcast(I32),
+            )
+        key_bytes = keep.tile([P, T], U8, name="key_bytes", align_bytes=64)
+        nc.vector.memset(key_bytes[:].bitcast(I32), 0)
+        key_words = keep.tile([P, T], U32, name="key_words", align_bytes=64)
+        nc.sync.dma_start(
+            out=key_words[:].bitcast(I32),
+            in_=keys_words[0].rearrange("p n t -> p (n t)").bitcast(I32),
+        )
+        idx = keep.tile([P, I // 16], U16, name="idx")
+        nc.sync.dma_start(idx[:], offs)
+        mem_cols = keep.tile([P, PACK], F32, name="mem_cols")
+        nc.sync.dma_start(out=mem_cols[:], in_=mem.rearrange("o (p c) -> p (o c)", c=PACK))
+        notes_v = notes.rearrange("(p t) u -> p t u", t=PACK)
+        notes_raw = []
+        for h in range(2):
+            raw = keep.tile([P, PACK, BANK], F32, name="notes_raw%d" % h)
+            nc.sync.dma_start(out=raw[:], in_=notes_v[:, :, h * BANK : (h + 1) * BANK])
+            notes_raw.append(raw)
+        idx3 = keep.tile([P, J // 16], U16, name="idx3")
+        nc.sync.dma_start(idx3[:], offs3)
+        users_v = users2.rearrange("(p t) z -> p t z", t=PACK)
+        users_raw = []
+        for t in range(PACK):
+            raw = keep.tile([P, Z], F32, name="users_raw%d" % t)
+            nc.sync.dma_start(out=raw[:], in_=users_v[:, t, :])
+            users_raw.append(raw)
+        idx2 = keep.tile([P, J // 16], U16, name="idx2")
+        nc.sync.dma_start(idx2[:], offs2)
+        row_factor = keep.tile([P, PACK], F32, name="row_factor")
+        nc.sync.dma_start(out=row_factor[:], in_=rowf.rearrange("(p r) o -> p (r o)", r=PACK))
+        vals_raw = []
+        for k in range(E // P):
+            raw = keep.tile([P, T], F32, name="vals_raw%d" % k)
+            nc.sync.dma_start(out=raw[:], in_=vals[k * P : (k + 1) * P, :])
+            vals_raw.append(raw)
+
+        ident = keep.tile([P, P], F32, name="ident")
+        make_identity(nc, ident[:])
+        before = []
+        for k in range(E // P):
+            tile = keep.tile([P, J], F32, name="before%d" % k, tag=("hold2", "before1", "hold3", "before3")[k], align_bytes=64)
+            nc.vector.memset(tile[:, 0:1], 0.0)
+            before.append(tile)
+
+        spread = psum.tile([P, PACK, P], F32, name="spread", tag="n3")
+        for c in range(PACK):
+            nc.tensor.transpose(spread[:, c, :], mem_cols[:, c : c + 1].to_broadcast([P, P]), ident[:])
+        mem_row = keep.tile([P, J], F32, name="mem_row")
+        nc.scalar.copy(mem_row[:].rearrange("p (n c) -> p n c", c=PACK), spread[:].rearrange("p c n -> p n c"))
+
+        for q in range(4):
+            rows = slice(32 * q, 32 * q + 4)
+            nc.vector.tensor_copy(key_bytes[rows, :].bitcast(I32), landed[rows, :])
+        kc = keep.tile([P, I], U32, name="kc", align_bytes=64)
+        nc.vector.tensor_copy(kc[:].rearrange("p (r s) -> p s r", r=PACK), key_words[:].indirect(idx[:]))
+        ks = keep.tile([P, I], U8, name="ks", align_bytes=64)
+        nc.vector.tensor_copy(ks[:].rearrange("p (r s) -> p s r", r=PACK), key_bytes[:].indirect(idx[:]))
+
+        def table_pass(r, codes, scales, tag):
+            bank = psum.tile([P, BANK], F32, name="bank", tag=tag)
+            cols = slice(r * P, (r + 1) * P)
+            nc.tensor.matmul_mx(
+                out=bank[:], lhsT=kc[:, cols].bitcast(FP8X4), lhsT_scale=ks[:, cols],
+                rhs=codes[:].bitcast(FP8X4), rhs_scale=scales[:], start=True, stop=True,
+            )
+            return bank
+
+        wide = [keep.tile([P, U], F32, name="wide%d" % r, tag="wide%d" % r) for r in range(PACK)]
+        half = BANK // 2
+        for h in range(2):
+            grouped = keep.tile([P, BANK, PACK], BF16, name="notes_g%d" % h, tag="weave", align_bytes=64)
+            nc.vector.tensor_copy(woven(grouped[:]), by_planes(notes_raw[h][:]))
+            codes, scales = quantise("notes%d" % h, grouped[:].rearrange("p u t -> p (u t)"), BANK)
+            for r in range(PACK):
+                bank = table_pass(r, codes, scales, "s%d" % r)
+                nc.scalar.copy(wide[r][:, h * BANK : (h + 1) * BANK], bank[:])
+
+        users_g = keep.tile([P, PACK, J], BF16, name="users_g", tag="weave", align_bytes=64)
+        for t in range(PACK):
+            nc.vector.tensor_copy(users_g[:, t, :], users_raw[t][:].indirect(idx3[:]))
+        users_w = keep.tile([P, J, PACK], BF16, name="users_w", align_bytes=64)
+        nc.vector.tensor_copy(woven(users_w[:]), by_planes(users_g[:]))
+        ucodes, uscales = quantise("users", users_w[:].rearrange("p u t -> p (u t)"), J)
+
+        picked = keep.tile([P, PACK, J], F32, name="picked", tag="hold0", align_bytes=64)
+        larger = keep.tile([P, PACK, J], F32, name="larger", tag="hold1", align_bytes=64)
+        for r in range(PACK):
+            nc.scalar.activation(picked[:, r, :], wide[r][:].indirect(idx2[:]), COPY)
+        for r in range(PACK):
+            narrow = table_pass(r, ucodes, uscales, "n%d" % r)
+            nc.vector.tensor_tensor(larger[:, r, :], picked[:, r, :], narrow[:], ALU.max)
+        table = keep.tile([P, J, PACK], BF16, name="table", align_bytes=64)
+        factor = row_factor[:].unsqueeze(1).unsqueeze(3).to_broadcast([P, half // 4, PACK, 4])
+        for h in range(2):
+            cols = slice(h * half, (h + 1) * half)
+            nc.vector.tensor_tensor(woven(table[:, cols, :]), by_planes(larger[:, :, cols]), factor, ALU.mult)
+        tcodes = keep.tile([P, J], U32, name="tcodes", align_bytes=64)
+        tscales = keep.tile([P, J], U8, name="tscales", align_bytes=64)
+        for h in range(2):
+            cols = slice(h * half, (h + 1) * half)
+            nc.vector.quantize_mx(
+                out=tcodes[:, cols].bitcast(FP8X4), scales=tscales[:, cols],
+                in_=table[:, cols, :].rearrange("p u t -> p (u t)"),
+            )
+
+        for k in range(E // P):
+            vg = keep.tile([P, I], BF16, name="vg%d" % k, tag="wide%d" % min(k, 2))
+            nc.scalar.activation(vg[:], vals_raw[k][:].indirect(idx[:]), COPY)
+            words = vg[:].bitcast(F32)
+            turned = psum.tile([P, 2, P], F32, name="turned", tag="n%d" % k)
+            for u in range(2):
+                nc.tensor.transpose(turned[:, u, :], words[:, u : I // 2 : 2], ident[:])
+            vw = keep.tile([P, P * PACK], BF16, name="vw%d" % k, align_bytes=64)
+            nc.scalar.copy(
+                vw[:].bitcast(F32).rearrange("p (e u) -> p e u", u=2), turned[:].rearrange("p u e -> p e u")
+            )
+            vcodes, vscales = quantise("vals%d" % k, vw[:], P, "hold%d" % k)
+            o = psum.tile([P, J], F32, name="o", tag="s%d" % k)
+            nc.tensor.matmul_mx(
+                out=o[:], lhsT=vcodes[:].bitcast(FP8X4), lhsT_scale=vscales[:],
+                rhs=tcodes[:].bitcast(FP8X4), rhs_scale=tscales[:], start=True, stop=True,
+            )
+            nc.vector.tensor_tensor(before[k][:, 1:J], o[:, 0 : J - 1], mem_row[:, 1:J], ALU.mult)
+            res = keep.tile([P, J], F32, name="res%d" % k)
+            nc.vector.tensor_tensor(res[:], o[:], before[k][:], ALU.subtract)
+            nc.sync.dma_start(out=out[k * P : (k + 1) * P, :], in_=res[:])

@@ -33,144 +33,213 @@ def tile_attend_tab_wideandown_changes_kernel(
     tc, keys_words, keys_scales, notes, users2, rowf, vals, mem, offs, offs2, offs3, out
 ):
     nc = tc.nc
+    half = J // 2
     with ExitStack() as ctx:
         keep = ctx.enter_context(tc.tile_pool(name="keep", bufs=1))
         psum = ctx.enter_context(tc.psum_pool(name="psum", bufs=1))
 
-        def quantise(name, grouped, cols, tag=""):
-            codes = keep.tile([P, cols], U32, name=name + "_codes", tag=tag, align_bytes=64)
-            scales = keep.tile([P, cols], U8, name=name + "_scales", align_bytes=64)
+        def sbuf(name, shape, dtype, slot=""):
+            return keep.tile(shape, dtype, name=name, tag=slot or name, align_bytes=64)
+
+        def load(name, shape, dtype, src, queue=nc.sync):
+            tile = sbuf(name, shape, dtype)
+            queue.dma_start(tile[:], src)
+            return tile
+
+        def quantise(name, grouped, cols, slot=""):
+            codes = sbuf(name + "_codes", [P, cols], U32, slot)
+            scales = sbuf(name + "_scales", [P, cols], U8)
             nc.vector.quantize_mx(out=codes[:].bitcast(FP8X4), scales=scales[:], in_=grouped)
-            return codes, scales
+            return codes[:], scales[:]
 
-        landed = keep.tile([P, T // 4], I32, name="landed")
-        for q in range(4):
-            nc.sync.dma_start(
-                out=landed[32 * q : 32 * q + 4, :],
-                in_=keys_scales[0][4 * q : 4 * q + 4, :].bitcast(I32),
+        def product(dst, left, right):
+            nc.tensor.matmul_mx(
+                out=dst, lhsT=left[0].bitcast(FP8X4), lhsT_scale=left[1],
+                rhs=right[0].bitcast(FP8X4), rhs_scale=right[1], start=True, stop=True,
             )
-        key_bytes = keep.tile([P, T], U8, name="key_bytes", align_bytes=64)
-        nc.vector.memset(key_bytes[:].bitcast(I32), 0)
-        key_words = keep.tile([P, T], U32, name="key_words", align_bytes=64)
-        nc.sync.dma_start(
-            out=key_words[:].bitcast(I32),
-            in_=keys_words[0].rearrange("p n t -> p (n t)").bitcast(I32),
-        )
-        idx = keep.tile([P, I // 16], U16, name="idx")
-        nc.sync.dma_start(idx[:], offs)
-        mem_cols = keep.tile([P, PACK], F32, name="mem_cols")
-        nc.sync.dma_start(out=mem_cols[:], in_=mem.rearrange("o (p c) -> p (o c)", c=PACK))
-        notes_v = notes.rearrange("(p t) u -> p t u", t=PACK)
-        notes_raw = []
-        for h in range(2):
-            raw = keep.tile([P, PACK, BANK], F32, name="notes_raw%d" % h)
-            nc.sync.dma_start(out=raw[:], in_=notes_v[:, :, h * BANK : (h + 1) * BANK])
-            notes_raw.append(raw)
-        idx3 = keep.tile([P, J // 16], U16, name="idx3")
-        nc.sync.dma_start(idx3[:], offs3)
-        users_v = users2.rearrange("(p t) z -> p t z", t=PACK)
-        users_raw = []
-        for t in range(PACK):
-            raw = keep.tile([P, Z], F32, name="users_raw%d" % t)
-            nc.sync.dma_start(out=raw[:], in_=users_v[:, t, :])
-            users_raw.append(raw)
-        idx2 = keep.tile([P, J // 16], U16, name="idx2")
-        nc.sync.dma_start(idx2[:], offs2)
-        row_factor = keep.tile([P, PACK], F32, name="row_factor")
-        nc.sync.dma_start(out=row_factor[:], in_=rowf.rearrange("(p r) o -> p (r o)", r=PACK))
-        vals_raw = []
-        for k in range(E // P):
-            raw = keep.tile([P, T], F32, name="vals_raw%d" % k)
-            nc.sync.dma_start(out=raw[:], in_=vals[k * P : (k + 1) * P, :])
-            vals_raw.append(raw)
 
-        ident = keep.tile([P, P], F32, name="ident")
+        landed = sbuf("landed", [P, T // 4], I32)
+        for q in range(4):
+            (nc.sync, nc.scalar)[q % 2].dma_start(
+                landed[32 * q : 32 * q + 4, :], keys_scales[0][4 * q : 4 * q + 4, :].bitcast(I32)
+            )
+        mem_cols = load("mem_cols", [P, PACK], F32, mem.rearrange("o (p c) -> p (o c)", c=PACK), nc.scalar)
+        row_factor = load("row_factor", [P, PACK], F32, rowf.rearrange("(p r) o -> p (r o)", r=PACK), nc.scalar)
+        idx = load("idx", [P, I // 16], U16, offs)
+        notes_v = notes.rearrange("(p t) u -> p t u", t=PACK)
+        edges = [0,256,512,768,1024]
+        spans = [slice(a, b) for a, b in zip(edges, edges[1:])]
+        widths = [s.stop - s.start for s in spans]
+
+        def load_notes(c):
+            return load("notes_raw%d" % c, [P, PACK, widths[c]], F32, notes_v[:, :, spans[c]])
+
+        notes_raw = [load_notes(0)]
+        key_words = sbuf("key_words", [P, T], U32, "chain")
+        nc.sync.dma_start(key_words[:].bitcast(I32), keys_words[0].rearrange("p n t -> p (n t)").bitcast(I32))
+        notes_raw.extend(load_notes(c) for c in range(1, len(spans)))
+        idx3 = load("idx3", [P, J // 16], U16, offs3)
+        users_v = users2.rearrange("(p t) z -> p t z", t=PACK)
+        users_raw = [load("users_raw%d" % t, [P, Z], F32, users_v[:, t, :]) for t in range(PACK)]
+        idx2 = load("idx2", [P, J // 16], U16, offs2)
+        vals_raw = [load("vals_raw%d" % k, [P, T], F32, vals[k * P : (k + 1) * P, :]) for k in range(E // P)]
+
+        key_bytes = sbuf("key_bytes", [P, T], U8)
+        nc.vector.memset(key_bytes[:].bitcast(I32), 0)
+        ident = sbuf("ident", [P, P], F32)
         make_identity(nc, ident[:])
-        before = []
-        for k in range(E // P):
-            tile = keep.tile([P, J], F32, name="before%d" % k, tag=("hold2", "before1", "hold3", "before3")[k], align_bytes=64)
-            nc.vector.memset(tile[:, 0:1], 0.0)
-            before.append(tile)
 
         spread = psum.tile([P, PACK, P], F32, name="spread", tag="n3")
         for c in range(PACK):
             nc.tensor.transpose(spread[:, c, :], mem_cols[:, c : c + 1].to_broadcast([P, P]), ident[:])
-        mem_row = keep.tile([P, J], F32, name="mem_row")
+        mem_row = sbuf("mem_row", [P, J], F32)
         nc.scalar.copy(mem_row[:].rearrange("p (n c) -> p n c", c=PACK), spread[:].rearrange("p c n -> p n c"))
 
         for q in range(4):
             rows = slice(32 * q, 32 * q + 4)
             nc.vector.tensor_copy(key_bytes[rows, :].bitcast(I32), landed[rows, :])
-        kc = keep.tile([P, I], U32, name="kc", align_bytes=64)
-        nc.vector.tensor_copy(kc[:].rearrange("p (r s) -> p s r", r=PACK), key_words[:].indirect(idx[:]))
-        ks = keep.tile([P, I], U8, name="ks", align_bytes=64)
+        ks = sbuf("ks", [P, I], U8)
         nc.vector.tensor_copy(ks[:].rearrange("p (r s) -> p s r", r=PACK), key_bytes[:].indirect(idx[:]))
 
-        def table_pass(r, codes, scales, tag):
-            bank = psum.tile([P, BANK], F32, name="bank", tag=tag)
-            cols = slice(r * P, (r + 1) * P)
-            nc.tensor.matmul_mx(
-                out=bank[:], lhsT=kc[:, cols].bitcast(FP8X4), lhsT_scale=ks[:, cols],
-                rhs=codes[:].bitcast(FP8X4), rhs_scale=scales[:], start=True, stop=True,
-            )
-            return bank
+        def weave_notes(c, slot, copy):
+            grouped = sbuf("notes_g%d" % c, [P, widths[c], PACK], BF16, slot)
+            copy(woven(grouped[:]), by_planes(notes_raw[c][:]))
+            return grouped[:].rearrange("p u t -> p (u t)")
 
-        wide = [keep.tile([P, U], F32, name="wide%d" % r, tag="wide%d" % r) for r in range(PACK)]
-        half = BANK // 2
-        for h in range(2):
-            grouped = keep.tile([P, BANK, PACK], BF16, name="notes_g%d" % h, tag="weave", align_bytes=64)
-            nc.vector.tensor_copy(woven(grouped[:]), by_planes(notes_raw[h][:]))
-            codes, scales = quantise("notes%d" % h, grouped[:].rearrange("p u t -> p (u t)"), BANK)
-            for r in range(PACK):
-                bank = table_pass(r, codes, scales, "s%d" % r)
-                nc.scalar.copy(wide[r][:, h * BANK : (h + 1) * BANK], bank[:])
+        notes_q = [quantise("notes0", weave_notes(0, "first", nc.vector.tensor_copy), widths[0])]
+        kc = sbuf("kc", [P, I], U32, "first")
+        nc.vector.tensor_copy(kc[:].rearrange("p (r s) -> p s r", r=PACK), key_words[:].indirect(idx[:]))
+        keys_q = [(kc[:, r * P : (r + 1) * P], ks[:, r * P : (r + 1) * P]) for r in range(PACK)]
+        second = weave_notes(1, "", nc.scalar.copy)
+        wide = sbuf("wide", [P, PACK * U], F32, "notes_raw1")
+        wide_rows = wide[:].rearrange("p (r u) -> p r u", r=PACK)
+        turn = [0]
 
-        users_g = keep.tile([P, PACK, J], BF16, name="users_g", tag="weave", align_bytes=64)
-        for t in range(PACK):
+        def wide_part(c):
+            per = BANK // widths[c]
+            for first in range(0, PACK, per):
+                bank = psum.tile([P, per, widths[c]], F32, name="bank", tag="s%d" % (turn[0] % 4))
+                turn.append(turn.pop() + 1)
+                for r in range(per):
+                    product(bank[:, r, :], keys_q[first + r], notes_q[c])
+                nc.scalar.copy(wide_rows[:, first : first + per, spans[c]], bank[:])
+
+        wide_part(0)
+        for c in range(1, len(spans)):
+            grouped = second if c == 1 else weave_notes(c, "chain" if c == 2 else "", nc.vector.tensor_copy)
+            notes_q.append(quantise("notes%d" % c, grouped, widths[c]))
+            wide_part(c)
+
+        users_g = sbuf("users_g", [P, PACK, J], BF16, "notes_g3")
+        cols = [slice(h * half, (h + 1) * half) for h in range(2)]
+        lists = [slice(h * half // 16, (h + 1) * half // 16) for h in range(2)]
+        for t in range(PACK - 1):
             nc.vector.tensor_copy(users_g[:, t, :], users_raw[t][:].indirect(idx3[:]))
-        users_w = keep.tile([P, J, PACK], BF16, name="users_w", align_bytes=64)
-        nc.vector.tensor_copy(woven(users_w[:]), by_planes(users_g[:]))
-        ucodes, uscales = quantise("users", users_w[:].rearrange("p u t -> p (u t)"), J)
+        nc.vector.tensor_copy(users_g[:, 3, cols[0]], users_raw[3][:].indirect(idx3[:, lists[0]]))
+        nc.scalar.activation(users_g[:, 3, cols[1]], users_raw[3][:].indirect(idx3[:, lists[1]]), COPY)
+        narrow = {}
+        for h in range(2):
+            users_w = sbuf("users_w%d" % h, [P, half, PACK], BF16, "")
+            nc.vector.tensor_copy(woven(users_w[:]), by_planes(users_g[:, :, cols[h]]))
+            users_q = quantise("users%d" % h, users_w[:].rearrange("p u t -> p (u t)"), half)
+            for pair in range(2):
+                bank = psum.tile([P, 2, half], F32, name="narrow", tag="n%d" % (2 * h + pair))
+                for r in range(2):
+                    product(bank[:, r, :], keys_q[2 * pair + r], users_q)
+                narrow[h, pair] = bank
 
-        picked = keep.tile([P, PACK, J], F32, name="picked", tag="hold0", align_bytes=64)
-        larger = keep.tile([P, PACK, J], F32, name="larger", tag="hold1", align_bytes=64)
-        for r in range(PACK):
-            nc.scalar.activation(picked[:, r, :], wide[r][:].indirect(idx2[:]), COPY)
-        for r in range(PACK):
-            narrow = table_pass(r, ucodes, uscales, "n%d" % r)
-            nc.vector.tensor_tensor(larger[:, r, :], picked[:, r, :], narrow[:], ALU.max)
-        table = keep.tile([P, J, PACK], BF16, name="table", align_bytes=64)
         factor = row_factor[:].unsqueeze(1).unsqueeze(3).to_broadcast([P, half // 4, PACK, 4])
+        picked = [sbuf("picked%d" % h, [P, PACK, half], F32, "users_w0" if h else "") for h in range(2)]
         for h in range(2):
-            cols = slice(h * half, (h + 1) * half)
-            nc.vector.tensor_tensor(woven(table[:, cols, :]), by_planes(larger[:, :, cols]), factor, ALU.mult)
-        tcodes = keep.tile([P, J], U32, name="tcodes", align_bytes=64)
-        tscales = keep.tile([P, J], U8, name="tscales", align_bytes=64)
-        for h in range(2):
-            cols = slice(h * half, (h + 1) * half)
+            for r in range(PACK):
+                window = wide[:, r * U : (r + 1) * U].indirect(idx2[:, lists[h]])
+                if h == 1 and r >= PACK - 2:
+                    nc.vector.tensor_copy(picked[h][:, r, :], window)
+                else:
+                    nc.scalar.activation(picked[h][:, r, :], window, COPY)
+
+        larger = [sbuf("larger%d" % h, [P, PACK, half], F32) for h in range(2)]
+        table = [sbuf("table%d" % h, [P, half, PACK], BF16) for h in range(2)]
+        tcodes = sbuf("tcodes", [P, J], U32)
+        tscales = sbuf("tscales", [P, J], U8)
+
+        def take_larger(h):
+            for pair in range(2):
+                rows = slice(2 * pair, 2 * pair + 2)
+                nc.vector.tensor_tensor(larger[h][:, rows, :], picked[h][:, rows, :], narrow[h, pair][:], ALU.max)
+
+        def weigh(h):
+            nc.vector.tensor_tensor(woven(table[h][:]), by_planes(larger[h][:]), factor, ALU.mult)
+
+        def quantise_table(h):
             nc.vector.quantize_mx(
-                out=tcodes[:, cols].bitcast(FP8X4), scales=tscales[:, cols],
-                in_=table[:, cols, :].rearrange("p u t -> p (u t)"),
+                out=tcodes[:, cols[h]].bitcast(FP8X4), scales=tscales[:, cols[h]],
+                in_=table[h][:].rearrange("p u t -> p (u t)"),
             )
 
-        for k in range(E // P):
-            vg = keep.tile([P, I], BF16, name="vg%d" % k, tag="wide%d" % min(k, 2))
+        def gather_values(k):
+            vg = sbuf("vg%d" % k, [P, I], BF16, "vg%d" % (k % 2))
             nc.scalar.activation(vg[:], vals_raw[k][:].indirect(idx[:]), COPY)
-            words = vg[:].bitcast(F32)
+            return vg
+
+        def turn_values(k):
+            words = gathered[k][:].bitcast(F32)
             turned = psum.tile([P, 2, P], F32, name="turned", tag="n%d" % k)
             for u in range(2):
                 nc.tensor.transpose(turned[:, u, :], words[:, u : I // 2 : 2], ident[:])
-            vw = keep.tile([P, P * PACK], BF16, name="vw%d" % k, align_bytes=64)
+            vw = sbuf("vw%d" % k, [P, P * PACK], BF16, "vals_raw%d" % (k + 1))
             nc.scalar.copy(
                 vw[:].bitcast(F32).rearrange("p (e u) -> p e u", u=2), turned[:].rearrange("p u e -> p e u")
             )
-            vcodes, vscales = quantise("vals%d" % k, vw[:], P, "hold%d" % k)
-            o = psum.tile([P, J], F32, name="o", tag="s%d" % k)
-            nc.tensor.matmul_mx(
-                out=o[:], lhsT=vcodes[:].bitcast(FP8X4), lhsT_scale=vscales[:],
-                rhs=tcodes[:].bitcast(FP8X4), rhs_scale=tscales[:], start=True, stop=True,
+            return vw
+
+        res = [sbuf("res%d" % k, [P, J], F32) for k in range(E // P)]
+        before = {}
+
+        def open_tile(k, slot):
+            before[k] = sbuf("before%d" % k, [P, J], F32, slot)
+            nc.vector.memset(before[k][:, 0:1], 0.0)
+
+        def finish(k, vq, lo, hi, tag):
+            o = psum.tile([P, hi - lo], F32, name="o", tag=tag)
+            product(o[:], vq, (tcodes[:, lo:hi], tscales[:, lo:hi]))
+            last = min(hi + 1, J)
+            nc.vector.tensor_tensor(
+                before[k][:, lo + 1 : last], o[:, : last - lo - 1], mem_row[:, lo + 1 : last], ALU.mult
             )
-            nc.vector.tensor_tensor(before[k][:, 1:J], o[:, 0 : J - 1], mem_row[:, 1:J], ALU.mult)
-            res = keep.tile([P, J], F32, name="res%d" % k)
-            nc.vector.tensor_tensor(res[:], o[:], before[k][:], ALU.subtract)
-            nc.sync.dma_start(out=out[k * P : (k + 1) * P, :], in_=res[:])
+            nc.vector.tensor_tensor(res[k][:, lo:hi], o[:], before[k][:, lo:hi], ALU.subtract)
+
+        def store(k, lo, hi):
+            nc.sync.dma_start(out[k * P : (k + 1) * P, lo:hi], res[k][:, lo:hi])
+
+        take_larger(0)
+        weigh(0)
+        take_larger(1)
+        quantise_table(0)
+        weigh(1)
+        gathered = [gather_values(0)]
+        turned_vals = []
+        for k in range(E // P):
+            if k + 1 < E // P:
+                gathered.append(gather_values(k + 1))
+            turned_vals.append(turn_values(k))
+        vq0 = quantise("vals0", turned_vals[0][:], P)
+        quantise_table(1)
+        vq1 = quantise("vals1", turned_vals[1][:], P)
+        open_tile(0, "vals_raw2")
+        finish(0, vq0, 0, half, "s0")
+        finish(0, vq0, half, J, "s1")
+        store(0, 0, J)
+        vq2 = quantise("vals2", turned_vals[2][:], P)
+        open_tile(1, "vals_raw3")
+        finish(1, vq1, 0, J, "s2")
+        store(1, 0, J)
+        vq3 = quantise("vals3", turned_vals[3][:], P)
+        open_tile(2, "vals_raw4")
+        finish(2, vq2, 0, J, "s3")
+        store(2, 0, J)
+        open_tile(3, "")
+        finish(3, vq3, 0, half, "s0")
+        store(3, 0, half)
+        finish(3, vq3, half, J, "s1")
+        store(3, half, J)

from contextlib import ExitStack

import concourse.mybir as mybir
from concourse.masks import make_identity

D, T, I, J, U, Z, E = 512, 2048, 512, 512, 1024, 1024, 512
FLOPS = 2 * D * I * U + 2 * D * I * J + 2 * I * E * J

F32 = mybir.dt.float32
BF16 = mybir.dt.bfloat16
I32 = mybir.dt.int32
U32 = mybir.dt.uint32
U16 = mybir.dt.uint16
U8 = mybir.dt.uint8
FP8X4 = mybir.dt.float8_e4m3fn_x4
ALU = mybir.AluOpType
COPY = mybir.ActivationFunctionType.Copy

P = 128
PACK = 4
BANK = 512


def woven(grouped):
    return grouped.rearrange("p (c i) t -> p c t i", i=4)


def by_planes(planes):
    return planes.rearrange("p t (c i) -> p c t i", i=4)


def tile_attend_tab_wideandown_changes_kernel(
    tc, keys_words, keys_scales, notes, users2, rowf, vals, mem, offs, offs2, offs3, out
):
    nc = tc.nc
    half = J // 2
    with ExitStack() as ctx:
        keep = ctx.enter_context(tc.tile_pool(name="keep", bufs=1))
        psum = ctx.enter_context(tc.psum_pool(name="psum", bufs=1))

        def sbuf(name, shape, dtype, slot=""):
            return keep.tile(shape, dtype, name=name, tag=slot or name, align_bytes=64)

        def load(name, shape, dtype, src, queue=nc.sync):
            tile = sbuf(name, shape, dtype)
            queue.dma_start(tile[:], src)
            return tile

        def quantise(name, grouped, cols, slot=""):
            codes = sbuf(name + "_codes", [P, cols], U32, slot)
            scales = sbuf(name + "_scales", [P, cols], U8)
            nc.vector.quantize_mx(out=codes[:].bitcast(FP8X4), scales=scales[:], in_=grouped)
            return codes[:], scales[:]

        def product(dst, left, right):
            nc.tensor.matmul_mx(
                out=dst, lhsT=left[0].bitcast(FP8X4), lhsT_scale=left[1],
                rhs=right[0].bitcast(FP8X4), rhs_scale=right[1], start=True, stop=True,
            )

        landed = sbuf("landed", [P, T // 4], I32)
        for q in range(4):
            (nc.sync, nc.scalar)[q % 2].dma_start(
                landed[32 * q : 32 * q + 4, :], keys_scales[0][4 * q : 4 * q + 4, :].bitcast(I32)
            )
        mem_cols = load("mem_cols", [P, PACK], F32, mem.rearrange("o (p c) -> p (o c)", c=PACK), nc.scalar)
        row_factor = load("row_factor", [P, PACK], F32, rowf.rearrange("(p r) o -> p (r o)", r=PACK), nc.scalar)
        idx = load("idx", [P, I // 16], U16, offs)
        notes_v = notes.rearrange("(p t) u -> p t u", t=PACK)
        edges = [0,256,512,768,1024]
        spans = [slice(a, b) for a, b in zip(edges, edges[1:])]
        widths = [s.stop - s.start for s in spans]

        def load_notes(c):
            return load("notes_raw%d" % c, [P, PACK, widths[c]], F32, notes_v[:, :, spans[c]])

        notes_raw = [load_notes(0)]
        key_words = sbuf("key_words", [P, T], U32, "chain")
        nc.sync.dma_start(key_words[:].bitcast(I32), keys_words[0].rearrange("p n t -> p (n t)").bitcast(I32))
        notes_raw.extend(load_notes(c) for c in range(1, len(spans)))
        idx3 = load("idx3", [P, J // 16], U16, offs3)
        users_v = users2.rearrange("(p t) z -> p t z", t=PACK)
        users_raw = [load("users_raw%d" % t, [P, Z], F32, users_v[:, t, :]) for t in range(PACK)]
        idx2 = load("idx2", [P, J // 16], U16, offs2)
        vals_raw = [load("vals_raw%d" % k, [P, T], F32, vals[k * P : (k + 1) * P, :]) for k in range(E // P)]

        key_bytes = sbuf("key_bytes", [P, T], U8)
        nc.vector.memset(key_bytes[:].bitcast(I32), 0)
        ident = sbuf("ident", [P, P], F32)
        make_identity(nc, ident[:])

        spread = psum.tile([P, PACK, P], F32, name="spread", tag="n3")
        for c in range(PACK):
            nc.tensor.transpose(spread[:, c, :], mem_cols[:, c : c + 1].to_broadcast([P, P]), ident[:])
        mem_row = sbuf("mem_row", [P, J], F32)
        nc.scalar.copy(mem_row[:].rearrange("p (n c) -> p n c", c=PACK), spread[:].rearrange("p c n -> p n c"))

        for q in range(4):
            rows = slice(32 * q, 32 * q + 4)
            nc.vector.tensor_copy(key_bytes[rows, :].bitcast(I32), landed[rows, :])
        ks = sbuf("ks", [P, I], U8)
        nc.vector.tensor_copy(ks[:].rearrange("p (r s) -> p s r", r=PACK), key_bytes[:].indirect(idx[:]))

        def weave_notes(c, slot, copy):
            grouped = sbuf("notes_g%d" % c, [P, widths[c], PACK], BF16, slot)
            copy(woven(grouped[:]), by_planes(notes_raw[c][:]))
            return grouped[:].rearrange("p u t -> p (u t)")

        notes_q = [quantise("notes0", weave_notes(0, "first", nc.vector.tensor_copy), widths[0])]
        kc = sbuf("kc", [P, I], U32, "first")
        nc.vector.tensor_copy(kc[:].rearrange("p (r s) -> p s r", r=PACK), key_words[:].indirect(idx[:]))
        keys_q = [(kc[:, r * P : (r + 1) * P], ks[:, r * P : (r + 1) * P]) for r in range(PACK)]
        second = weave_notes(1, "", nc.scalar.copy)
        wide = sbuf("wide", [P, PACK * U], F32, "notes_raw1")
        wide_rows = wide[:].rearrange("p (r u) -> p r u", r=PACK)
        turn = [0]

        def wide_part(c):
            per = BANK // widths[c]
            for first in range(0, PACK, per):
                bank = psum.tile([P, per, widths[c]], F32, name="bank", tag="s%d" % (turn[0] % 4))
                turn.append(turn.pop() + 1)
                for r in range(per):
                    product(bank[:, r, :], keys_q[first + r], notes_q[c])
                nc.scalar.copy(wide_rows[:, first : first + per, spans[c]], bank[:])

        wide_part(0)
        for c in range(1, len(spans)):
            grouped = second if c == 1 else weave_notes(c, "chain" if c == 2 else "", nc.vector.tensor_copy)
            notes_q.append(quantise("notes%d" % c, grouped, widths[c]))
            wide_part(c)

        users_g = sbuf("users_g", [P, PACK, J], BF16, "notes_g3")
        cols = [slice(h * half, (h + 1) * half) for h in range(2)]
        lists = [slice(h * half // 16, (h + 1) * half // 16) for h in range(2)]
        for t in range(PACK - 1):
            nc.vector.tensor_copy(users_g[:, t, :], users_raw[t][:].indirect(idx3[:]))
        nc.vector.tensor_copy(users_g[:, 3, cols[0]], users_raw[3][:].indirect(idx3[:, lists[0]]))
        nc.scalar.activation(users_g[:, 3, cols[1]], users_raw[3][:].indirect(idx3[:, lists[1]]), COPY)
        narrow = {}
        for h in range(2):
            users_w = sbuf("users_w%d" % h, [P, half, PACK], BF16, "")
            nc.vector.tensor_copy(woven(users_w[:]), by_planes(users_g[:, :, cols[h]]))
            users_q = quantise("users%d" % h, users_w[:].rearrange("p u t -> p (u t)"), half)
            for pair in range(2):
                bank = psum.tile([P, 2, half], F32, name="narrow", tag="n%d" % (2 * h + pair))
                for r in range(2):
                    product(bank[:, r, :], keys_q[2 * pair + r], users_q)
                narrow[h, pair] = bank

        factor = row_factor[:].unsqueeze(1).unsqueeze(3).to_broadcast([P, half // 4, PACK, 4])
        picked = [sbuf("picked%d" % h, [P, PACK, half], F32, "users_w0" if h else "") for h in range(2)]
        for h in range(2):
            for r in range(PACK):
                window = wide[:, r * U : (r + 1) * U].indirect(idx2[:, lists[h]])
                if h == 1 and r >= PACK - 2:
                    nc.vector.tensor_copy(picked[h][:, r, :], window)
                else:
                    nc.scalar.activation(picked[h][:, r, :], window, COPY)

        larger = [sbuf("larger%d" % h, [P, PACK, half], F32) for h in range(2)]
        table = [sbuf("table%d" % h, [P, half, PACK], BF16) for h in range(2)]
        tcodes = sbuf("tcodes", [P, J], U32)
        tscales = sbuf("tscales", [P, J], U8)

        def take_larger(h):
            for pair in range(2):
                rows = slice(2 * pair, 2 * pair + 2)
                nc.vector.tensor_tensor(larger[h][:, rows, :], picked[h][:, rows, :], narrow[h, pair][:], ALU.max)

        def weigh(h):
            nc.vector.tensor_tensor(woven(table[h][:]), by_planes(larger[h][:]), factor, ALU.mult)

        def quantise_table(h):
            nc.vector.quantize_mx(
                out=tcodes[:, cols[h]].bitcast(FP8X4), scales=tscales[:, cols[h]],
                in_=table[h][:].rearrange("p u t -> p (u t)"),
            )

        def gather_values(k):
            vg = sbuf("vg%d" % k, [P, I], BF16, "vg%d" % (k % 2))
            nc.scalar.activation(vg[:], vals_raw[k][:].indirect(idx[:]), COPY)
            return vg

        def turn_values(k):
            words = gathered[k][:].bitcast(F32)
            turned = psum.tile([P, 2, P], F32, name="turned", tag="n%d" % k)
            for u in range(2):
                nc.tensor.transpose(turned[:, u, :], words[:, u : I // 2 : 2], ident[:])
            vw = sbuf("vw%d" % k, [P, P * PACK], BF16, "vals_raw%d" % (k + 1))
            nc.scalar.copy(
                vw[:].bitcast(F32).rearrange("p (e u) -> p e u", u=2), turned[:].rearrange("p u e -> p e u")
            )
            return vw

        res = [sbuf("res%d" % k, [P, J], F32) for k in range(E // P)]
        before = {}

        def open_tile(k, slot):
            before[k] = sbuf("before%d" % k, [P, J], F32, slot)
            nc.vector.memset(before[k][:, 0:1], 0.0)

        def finish(k, vq, lo, hi, tag):
            o = psum.tile([P, hi - lo], F32, name="o", tag=tag)
            product(o[:], vq, (tcodes[:, lo:hi], tscales[:, lo:hi]))
            last = min(hi + 1, J)
            nc.vector.tensor_tensor(
                before[k][:, lo + 1 : last], o[:, : last - lo - 1], mem_row[:, lo + 1 : last], ALU.mult
            )
            nc.vector.tensor_tensor(res[k][:, lo:hi], o[:], before[k][:, lo:hi], ALU.subtract)

        def store(k, lo, hi):
            nc.sync.dma_start(out[k * P : (k + 1) * P, lo:hi], res[k][:, lo:hi])

        take_larger(0)
        weigh(0)
        take_larger(1)
        quantise_table(0)
        weigh(1)
        gathered = [gather_values(0)]
        turned_vals = []
        for k in range(E // P):
            if k + 1 < E // P:
                gathered.append(gather_values(k + 1))
            turned_vals.append(turn_values(k))
        vq0 = quantise("vals0", turned_vals[0][:], P)
        quantise_table(1)
        vq1 = quantise("vals1", turned_vals[1][:], P)
        open_tile(0, "vals_raw2")
        finish(0, vq0, 0, half, "s0")
        finish(0, vq0, half, J, "s1")
        store(0, 0, J)
        vq2 = quantise("vals2", turned_vals[2][:], P)
        open_tile(1, "vals_raw3")
        finish(1, vq1, 0, J, "s2")
        store(1, 0, J)
        vq3 = quantise("vals3", turned_vals[3][:], P)
        open_tile(2, "vals_raw4")
        finish(2, vq2, 0, J, "s3")
        store(2, 0, J)
        open_tile(3, "")
        finish(3, vq3, 0, half, "s0")
        store(3, 0, half)
        finish(3, vq3, half, J, "s1")
        store(3, half, J)
